import numpy as np
import ml_dtypes


def mxq(x, axis, fmt="e4m3"):
    dtype, down = {"e4m3": (ml_dtypes.float8_e4m3fn, 7), "e5m2": (ml_dtypes.float8_e5m2, 14)}[fmt]
    v = np.moveaxis(np.asarray(x, np.float32).astype(ml_dtypes.bfloat16).astype(np.float64), axis, -1)
    blocks = v.reshape(v.shape[:-1] + (-1, 32))
    amax = np.abs(blocks).max(-1, keepdims=True)
    byte = np.maximum(np.where(amax > 0, np.frexp(amax)[1] - 1 + 127, 0) - down, 1)
    scale = np.exp2(byte - 127.0)
    codes = (blocks / scale).astype(np.float32).astype(dtype).astype(np.float64)
    return np.moveaxis((codes * scale).reshape(v.shape), -1, axis)


WIDE = False


def mx_kscale(k):
    if not WIDE:
        return np.ones(k)
    levels = np.array([10, -10, 5, -5, 0])
    if k % 512:
        return np.exp2(np.random.permutation(np.resize(levels, k // 32))).repeat(32)
    a = np.empty((k // 512, 16))
    for p in range(k // 512):
        a[p, :8] = np.random.permutation(np.resize(levels, 8))
        for g in range(8):
            far = levels[np.abs(levels - a[p, g]) >= 10]
            a[p, g + 8] = far[np.random.randint(len(far))]
    return np.exp2(a.ravel()).repeat(32)


def f64(x):
    return np.asarray(x).astype(np.float64)


def striped(idx):
    return np.tile(idx.reshape(-1, 16).T, (8, 1)).astype(np.uint16)


def unstriped(offs):
    return offs[:16].T.reshape(-1).astype(np.int64)


E2M1 = np.array([0.0, 0.5, 1.0, 1.5, 2.0, 3.0, 4.0, 6.0, -0.0, -0.5, -1.0, -1.5, -2.0, -3.0, -4.0, -6.0])


def pack_weight(w, fmt):
    k, n = w.shape
    w = f64(np.asarray(w, np.float32).astype(ml_dtypes.bfloat16)).reshape(k // 32, 32, n)
    amax = np.abs(w).max(1)
    if fmt == "e4m3":
        byte = np.frexp(amax)[1] - 1 + 127 - 7
    else:
        mant, ex = np.frexp(amax / 6.0)
        byte = np.where(mant > 0.5, ex, ex - 1) + 127
    byte = np.clip(np.where(amax > 0, byte, 1), 1, 254)
    scaled = (w * np.exp2(127.0 - byte)[:, None, :]).reshape(k, n).astype(np.float32)
    by_word = np.ascontiguousarray(scaled.reshape(k // 512, 128, 4, n).transpose(0, 1, 3, 2))
    if fmt == "e4m3":
        words = by_word.astype(ml_dtypes.float8_e4m3fn).view(np.uint8)
    else:
        c = by_word.astype(ml_dtypes.float4_e2m1fn).view(np.uint8) & 0xF
        words = (c[..., 0::2] | (c[..., 1::2] << 4)).reshape(k // 512, 128, 2 * n)
    return np.ascontiguousarray(words), np.ascontiguousarray(byte.astype(np.uint8).reshape(k // 512, 16, n))


def unpack_weight(words, scales, fmt):
    g, _, n = scales.shape
    words = np.ascontiguousarray(words).reshape(g, 128, n, -1)
    if fmt == "e4m3":
        vals = words.view(ml_dtypes.float8_e4m3fn).astype(np.float64)
    else:
        nib = np.empty((g, 128, n, 4), np.uint8)
        nib[..., 0::2] = words & 0xF
        nib[..., 1::2] = words >> 4
        vals = E2M1[nib]
    vals = vals * np.repeat(np.exp2(scales.astype(np.float64) - 127.0), 8, axis=1)[..., None]
    return vals.transpose(0, 1, 3, 2).reshape(g * 512, n)


def gelu(v):
    return 0.5 * v * (1.0 + np.tanh(np.sqrt(2.0 / np.pi) * (v + 0.044715 * v**3)))


def bf(x):
    return np.asarray(x, np.float32).astype(ml_dtypes.bfloat16)


def planes(Y):
    n, m = Y.shape
    b = f64(bf(Y)).reshape(n // 32, 32, m)
    amax = np.abs(b).max(1)
    byte = np.clip(np.where(amax > 0, np.frexp(amax)[1] - 1 + 127 - 7, 1), 1, 254)
    codes = (b * np.exp2(127.0 - byte)[:, None, :]).reshape(n, m).astype(np.float32).astype(ml_dtypes.float8_e4m3fn).view(np.uint8)
    words = codes.reshape(n // 512, 128, 4, m).transpose(0, 1, 3, 2)
    return np.ascontiguousarray(words), np.ascontiguousarray(byte.astype(np.uint8).reshape(n // 512, 16, m))


K, T, S, H, N, P = 1024, 4096, 1024, 1536, 512, 512

def setup_inputs():
    n = np.random.standard_normal
    s = mx_kscale(K)[:, None]
    u = mx_kscale(H)[:, None]
    tab_words, tab_scales = pack_weight(n((K, T)) * s, "e4m3")
    wa_words, wa_scales = pack_weight(n((H, N)) / np.sqrt(H) / u, "e2m1")
    w1 = (n((K, H)) / np.sqrt(K) / s).astype(np.float32)
    b1 = (0.6 * n(H)).astype(np.float32)
    gh = (np.random.uniform(0.7, 1.6, H) * u[:, 0]).astype(np.float32)
    side = np.where(n(N) > 0, 1.0, -1.0)
    gy = (4.0 * side * np.exp(0.8 * n(N))).astype(np.float32)
    return {"tab_words": tab_words, "tab_scales": tab_scales,
            "offs": striped(np.random.permutation(T)[:S]),
            "w1": w1, "b1": b1, "gh": gh,
            "wa_words": wa_words, "wa_scales": wa_scales,
            "pos1": striped(np.random.permutation(S)[:P]),
            "pos2": striped(np.random.permutation(S)[:P]),
            "gy": gy}

def reference(tab_words, tab_scales, offs, w1, b1, gh, wa_words, wa_scales, pos1, pos2, gy):
    v = unpack_weight(tab_words, tab_scales, "e4m3")[:, unstriped(offs)]
    w1q = mxq(f64(w1), 0, "e4m3")
    h = f64(gh)[:, None] * np.tanh((w1q.T @ v) + f64(b1)[:, None])
    hq = mxq(h, 0, "e4m3")
    wa = unpack_weight(wa_words, wa_scales, "e2m1")
    e = wa.T @ hq
    top = e.max(axis=1)
    a = np.exp(e[:, unstriped(pos1)] - top[:, None])
    c = e[:, unstriped(pos2)]
    y = f64(gy)[:, None] * a * c
    words, scales = planes(y)
    return y, words, scales

@@ -1,0 +1,279 @@
+from contextlib import ExitStack
+
+import concourse.mybir as mybir
+
+K, T, S, H, N, M = 1024, 4096, 1024, 1536, 512, 512
+FLOPS = 2 * K * H * S + 2 * H * N * S
+
+F32 = mybir.dt.float32
+BF16 = mybir.dt.bfloat16
+I32 = mybir.dt.int32
+U32 = mybir.dt.uint32
+U16 = mybir.dt.uint16
+U8 = mybir.dt.uint8
+FP8X4 = mybir.dt.float8_e4m3fn_x4
+FP4X4 = mybir.dt.float4_e2m1fn_x4
+ALU = mybir.AluOpType
+ACT = mybir.ActivationFunctionType
+
+P = 128
+PACK = 4
+PASS = P * PACK
+KP = K // PASS
+HP = H // PASS
+COLS = 512
+SH = S // COLS
+MC = 256
+MH = M // MC
+QUADS = 4
+
+
+def tile_list_burst_quiet_board_kernel(
+    tc, tab_words, tab_scales, offs, w1, b1, gh, wa_words, wa_scales, pos1, pos2, gy, out_0, out_1, out_2
+):
+    nc = tc.nc
+    with ExitStack() as ctx:
+        lists = ctx.enter_context(tc.tile_pool(name="lists", bufs=1))
+        keep = ctx.enter_context(tc.tile_pool(name="keep", bufs=1))
+        ring = ctx.enter_context(tc.tile_pool(name="ring", bufs=3))
+        psum = ctx.enter_context(tc.psum_pool(name="psum", bufs=4))
+
+        idx = lists.tile([P, S // 16], U16, name="idx")
+        p1 = lists.tile([P, M // 16], U16, name="p1")
+        p2 = lists.tile([P, M // 16], U16, name="p2")
+
+        tab_w = [keep.tile([P, T], I32, name=f"tab_w{a}") for a in range(KP)]
+        tab_s = keep.tile([P, T], U8, name="tab_s")
+        wa_w_raw = keep.tile([P, HP, 2 * N], U8, name="wa_w_raw")
+        wa_s_raw = keep.tile([P, HP, N], U8, name="wa_s_raw")
+        wa_w = keep.tile([P, HP, 2 * N], U8, name="wa_w", align_bytes=64)
+        wa_s = keep.tile([P, HP, N], U8, name="wa_s", align_bytes=64)
+        bias = keep.tile([P, HP, PACK], F32, name="bias")
+        gain = keep.tile([P, HP, PACK], F32, name="gain")
+        board = keep.tile([P, PACK], F32, name="board")
+        w_raw = {(b, a): keep.tile([P, PACK, PASS], F32, name=f"w_raw{b}{a}") for b in range(HP) for a in range(KP)}
+
+        nc.vector.memset(tab_s[:].bitcast(I32), 0)
+        nc.vector.memset(wa_s_raw[:].bitcast(I32), 0)
+
+        def load_w1(b, a, pieces):
+            rows = w1[a * PASS : (a + 1) * PASS, b * PASS : (b + 1) * PASS].rearrange("(p j) c -> p j c", j=PACK)
+            step = PACK // pieces
+            for j in range(0, PACK, step):
+                nc.sync.dma_start(out=w_raw[b, a][:, j : j + step, :], in_=rows[:, j : j + step, :])
+
+        def load_tab_scales(a, q):
+            nc.sync.dma_start(
+                out=tab_s[32 * q + 4 * a : 32 * q + 4 * a + 4, :].bitcast(I32),
+                in_=tab_scales[a, 4 * q : 4 * q + 4, :].bitcast(I32),
+            )
+
+        def load_tab_words(a, cols):
+            words = tab_words[a].rearrange("p t i -> p (t i)").bitcast(I32)
+            nc.sync.dma_start(out=tab_w[a][:, cols], in_=words[:, cols])
+
+        nc.gpsimd.dma_start(out=bias[:], in_=b1.rearrange("(b p t) -> p b t", p=P, t=PACK))
+        nc.gpsimd.dma_start(out=gain[:], in_=gh.rearrange("(b p t) -> p b t", p=P, t=PACK))
+        nc.gpsimd.dma_start(out=board[:], in_=gy.rearrange("(p t) -> p t", t=PACK))
+
+        nc.sync.dma_start(idx[:], offs)
+        load_w1(0, 0, 4)
+        wa_rows = wa_words.rearrange("a p c -> p a c").bitcast(I32)
+        nc.sync.dma_start(out=wa_w_raw[:, :2, :].bitcast(I32), in_=wa_rows[:, :2, :])
+        nc.sync.dma_start(out=wa_w_raw[:, 2:, :].bitcast(I32), in_=wa_rows[:, 2:, :])
+        load_w1(0, 1, 1)
+        scale_rows = [(a, q) for a in range(KP) for q in range(QUADS)]
+        for a, q in scale_rows[:6]:
+            load_tab_scales(a, q)
+        load_tab_words(0, slice(0, T // 2))
+        for a, q in scale_rows[6:]:
+            load_tab_scales(a, q)
+        for q in range(QUADS):
+            nc.sync.dma_start(
+                out=wa_s_raw[32 * q : 32 * q + 4, :, :].bitcast(I32),
+                in_=wa_scales[:, 4 * q : 4 * q + 4, :].rearrange("a r n -> r a n").bitcast(I32),
+            )
+        load_tab_words(0, slice(T // 2, T))
+        load_tab_words(1, slice(0, T))
+        for b in range(1, HP):
+            for a in range(KP):
+                load_w1(b, a, 1)
+        nc.sync.dma_start(p1[:], pos1)
+        nc.sync.dma_start(p2[:], pos2)
+
+        w_b, w_q, w_s = {}, {}, {}
+
+        def round_w1(b, a, on_vector):
+            w_b[b, a] = ring.tile([P, PACK * PASS], BF16, name="w_b", align_bytes=64)
+            dst = w_b[b, a][:].rearrange("p (g u m j) -> p g m j u", g=2, u=2, j=PACK)
+            src = w_raw[b, a][:].rearrange("p j (m g u) -> p g m j u", g=2, u=2)
+            if on_vector == 2:
+                nc.vector.tensor_copy(out=dst, in_=src)
+            elif on_vector == 1:
+                nc.vector.tensor_copy(out=dst[:, 0], in_=src[:, 0])
+                nc.scalar.copy(out=dst[:, 1], in_=src[:, 1])
+            else:
+                nc.scalar.copy(out=dst, in_=src)
+
+        def quantise_w1(b, a):
+            w_q[b, a] = keep.tile([P, PASS], U32, name=f"w_q{b}{a}", align_bytes=64)
+            w_s[b, a] = keep.tile([P, PASS], U8, name=f"w_s{b}{a}", align_bytes=64)
+            nc.vector.quantize_mx(out=w_q[b, a][:].bitcast(FP8X4), scales=w_s[b, a][:], in_=w_b[b, a][:])
+
+        round_w1(0, 0, 0)
+        round_w1(0, 1, 0)
+        quantise_w1(0, 0)
+        nc.vector.tensor_copy(
+            out=wa_w[:].bitcast(U16).rearrange("p a (t m) -> p a m t", t=PACK),
+            in_=wa_w_raw[:].bitcast(U16).rearrange("p a (m t) -> p a m t", t=PACK),
+        )
+        quantise_w1(0, 1)
+
+        v_s = keep.tile([P, S], U8, name="v_s", align_bytes=64)
+        nc.vector.tensor_copy(out=v_s[:], in_=tab_s[:].indirect(idx[:]))
+        v_w = {}
+        for a in range(KP):
+            for s in range(SH):
+                v_w[a, s] = keep.tile([P, COLS], U32, name=f"v_w{a}{s}", align_bytes=64)
+                entries = idx[:, s * COLS // 16 : (s + 1) * COLS // 16]
+                nc.vector.tensor_copy(out=v_w[a, s][:], in_=tab_w[a][:].bitcast(U32).indirect(entries))
+            if a == 0:
+                nc.vector.tensor_copy(
+                    out=wa_s[:].rearrange("p a (t m) -> p a m t", t=PACK),
+                    in_=wa_s_raw[:].rearrange("p a (m t) -> p a m t", t=PACK),
+                )
+
+        act, h_b, h_q, h_s = {}, {}, {}, {}
+
+        def first_stage(b, s):
+            act[b, s] = ring.tile([P, PACK, COLS], F32, name="act")
+            for t in range(PACK):
+                acc = psum.tile([P, COLS], F32, name="acc")
+                for a in range(KP):
+                    nc.tensor.matmul_mx(
+                        out=acc[:],
+                        lhsT=w_q[b, a][:, t * P : (t + 1) * P].bitcast(FP8X4),
+                        lhsT_scale=w_s[b, a][:, t * P : (t + 1) * P],
+                        rhs=v_w[a, s][:].bitcast(FP8X4),
+                        rhs_scale=v_s[4 * a : P, s * COLS : (s + 1) * COLS],
+                        start=(a == 0),
+                        stop=(a == KP - 1),
+                    )
+                nc.scalar.activation(out=act[b, s][:, t, :], in_=acc[:], func=ACT.Tanh, bias=bias[:, b, t : t + 1])
+
+        def round_h(b, s):
+            h_b[b, s] = ring.tile([P, PACK * COLS], BF16, name="h_b", align_bytes=64)
+            nc.vector.tensor_tensor(
+                out=h_b[b, s][:].rearrange("p (c i t) -> p c t i", i=2, t=PACK),
+                in0=act[b, s][:].rearrange("p t (c i) -> p c t i", i=2),
+                in1=gain[:, b, :].unsqueeze(1).unsqueeze(3).broadcast_to([P, COLS // 2, PACK, 2]),
+                op=ALU.mult,
+            )
+
+        def quantise_h(b, s):
+            h_q[b, s] = keep.tile([P, COLS], U32, name=f"h_q{b}{s}", align_bytes=64)
+            h_s[b, s] = keep.tile([P, COLS], U8, name=f"h_s{b}{s}", align_bytes=64)
+            nc.vector.quantize_mx(out=h_q[b, s][:].bitcast(FP8X4), scales=h_s[b, s][:], in_=h_b[b, s][:])
+
+        score = {}
+
+        def second_stage(b, s, t):
+            if b == 0:
+                score[s, t] = psum.tile([P, COLS], F32, name="score")
+            nc.tensor.matmul_mx(
+                out=score[s, t][:],
+                lhsT=wa_w[:, b, 2 * t * P : 2 * (t + 1) * P].bitcast(FP4X4),
+                lhsT_scale=wa_s[:, b, t * P : (t + 1) * P],
+                rhs=h_q[b, s][:].bitcast(FP8X4),
+                rhs_scale=h_s[b, s][:],
+                start=(b == 0),
+                stop=(b == HP - 1),
+            )
+
+        first_stage(0, 0)
+        round_w1(1, 0, 2)
+        first_stage(0, 1)
+        quantise_w1(1, 0)
+        round_h(0, 0)
+        round_w1(1, 1, 1)
+        quantise_h(0, 0)
+        round_w1(2, 0, 0)
+        quantise_w1(1, 1)
+        round_h(0, 1)
+        first_stage(1, 0)
+        for t in range(PACK):
+            second_stage(0, 0, t)
+        quantise_h(0, 1)
+        round_w1(2, 1, 0)
+        quantise_w1(2, 0)
+        round_h(1, 0)
+        first_stage(1, 1)
+        quantise_w1(2, 1)
+        quantise_h(1, 0)
+        first_stage(2, 0)
+        for t in range(PACK):
+            second_stage(1, 0, t)
+        round_h(1, 1)
+        first_stage(2, 1)
+        quantise_h(1, 1)
+        round_h(2, 0)
+        quantise_h(2, 0)
+        for t in range(PACK):
+            second_stage(2, 0, t)
+        round_h(2, 1)
+        quantise_h(2, 1)
+
+        e = [keep.tile([P, S], F32, name=f"e{t}") for t in range(PACK)]
+        peak = keep.tile([P, SH, PACK], F32, name="peak")
+        minus_peak = keep.tile([P, PACK], F32, name="minus_peak")
+
+        def keep_scores(s, t):
+            nc.vector.tensor_scalar(
+                out=e[t][:, s * COLS : (s + 1) * COLS],
+                in0=score[s, t][:],
+                scalar1=1.0,
+                scalar2=None if s == 0 else peak[:, s - 1, t : t + 1],
+                op0=ALU.mult,
+                op1=ALU.max,
+                accum_out=peak[:, s, t : t + 1],
+            )
+
+        for t in range(PACK):
+            keep_scores(0, t)
+            for b in range(HP):
+                second_stage(b, 1, t)
+        for t in range(PACK):
+            keep_scores(1, t)
+            nc.scalar.mul(out=minus_peak[:, t : t + 1], in_=peak[:, SH - 1, t : t + 1], mul=-1.0)
+
+        y_q = keep.tile([P, M], I32, name="y_q", align_bytes=64)
+        y_s = keep.tile([P, M], U8, name="y_s", align_bytes=64)
+        y_rows = out_0.rearrange("(p t) m -> p t m", t=PACK)
+        y_words = out_1[0].rearrange("p m t -> p (m t)").bitcast(I32)
+        for c in range(MH):
+            cols = slice(c * MC, (c + 1) * MC)
+            entries = slice(c * MC // 16, (c + 1) * MC // 16)
+            y = keep.tile([P, PACK, MC], F32, name=f"y{c}")
+            for t in range(PACK):
+                burst = ring.tile([P, MC], F32, name="burst")
+                scaled = ring.tile([P, MC], F32, name="scaled")
+                nc.scalar.activation(
+                    out=burst[:], in_=e[t][:].indirect(p1[:, entries]), func=ACT.Exp, bias=minus_peak[:, t : t + 1]
+                )
+                nc.scalar.activation(out=scaled[:], in_=burst[:], func=ACT.Copy, scale=board[:, t : t + 1])
+                nc.vector.tensor_tensor(
+                    out=y[:, t, :], in0=e[t][:].indirect(p2[:, entries]), in1=scaled[:], op=ALU.mult
+                )
+            nc.sync.dma_start(out=y_rows[:, :, cols], in_=y[:])
+            y_b = keep.tile([P, PACK * MC], BF16, name=f"y_b{c}", align_bytes=64)
+            nc.vector.tensor_copy(
+                out=y_b[:].rearrange("p (c i t) -> p c t i", i=2, t=PACK),
+                in_=y[:].rearrange("p t (c i) -> p c t i", i=2),
+            )
+            nc.vector.quantize_mx(out=y_q[:, cols].bitcast(FP8X4), scales=y_s[:, cols], in_=y_b[:])
+            nc.sync.dma_start(out=y_words[:, cols], in_=y_q[:, cols])
+        for q in range(QUADS):
+            queue = nc.sync if q % 2 == 0 else nc.scalar
+            queue.dma_start(
+                out=out_2[0, 4 * q : 4 * q + 4, :].bitcast(I32), in_=y_s[32 * q : 32 * q + 4, :].bitcast(I32)
+            )

@@ -62,19 +62,15 @@ def tile_list_burst_quiet_board_kernel(
             for j in range(0, PACK, step):
                 nc.sync.dma_start(out=w_raw[b, a][:, j : j + step, :], in_=rows[:, j : j + step, :])
 
-        def load_tab_scales(a, q):
+        def load_tab_scales(a, r):
             nc.sync.dma_start(
-                out=tab_s[32 * q + 4 * a : 32 * q + 4 * a + 4, :].bitcast(I32),
-                in_=tab_scales[a, 4 * q : 4 * q + 4, :].bitcast(I32),
+                out=tab_s[4 * a + r : P : 32, :].bitcast(I32),
+                in_=tab_scales[a, r : 16 : 4, :].bitcast(I32),
             )
 
         def load_tab_words(a, cols):
             words = tab_words[a].rearrange("p t i -> p (t i)").bitcast(I32)
             nc.sync.dma_start(out=tab_w[a][:, cols], in_=words[:, cols])
-
-        nc.gpsimd.dma_start(out=bias[:], in_=b1.rearrange("(b p t) -> p b t", p=P, t=PACK))
-        nc.gpsimd.dma_start(out=gain[:], in_=gh.rearrange("(b p t) -> p b t", p=P, t=PACK))
-        nc.gpsimd.dma_start(out=board[:], in_=gy.rearrange("(p t) -> p t", t=PACK))
 
         nc.sync.dma_start(idx[:], offs)
         load_w1(0, 0, 4)
@@ -82,22 +78,25 @@ def tile_list_burst_quiet_board_kernel(
         nc.sync.dma_start(out=wa_w_raw[:, :2, :].bitcast(I32), in_=wa_rows[:, :2, :])
         nc.sync.dma_start(out=wa_w_raw[:, 2:, :].bitcast(I32), in_=wa_rows[:, 2:, :])
         load_w1(0, 1, 1)
-        scale_rows = [(a, q) for a in range(KP) for q in range(QUADS)]
+        scale_rows = [(a, r) for r in range(4) for a in range(KP)]
         for a, q in scale_rows[:6]:
             load_tab_scales(a, q)
         load_tab_words(0, slice(0, T // 2))
         for a, q in scale_rows[6:]:
             load_tab_scales(a, q)
-        for q in range(QUADS):
+        for r in range(4):
             nc.sync.dma_start(
-                out=wa_s_raw[32 * q : 32 * q + 4, :, :].bitcast(I32),
-                in_=wa_scales[:, 4 * q : 4 * q + 4, :].rearrange("a r n -> r a n").bitcast(I32),
+                out=wa_s_raw[r:P:32, :, :].bitcast(I32),
+                in_=wa_scales[:, r:16:4, :].rearrange("a q n -> q a n").bitcast(I32),
             )
         load_tab_words(0, slice(T // 2, T))
         load_tab_words(1, slice(0, T))
+        nc.sync.dma_start(out=bias[:], in_=b1.rearrange("(b p t) -> p b t", p=P, t=PACK))
+        nc.sync.dma_start(out=gain[:], in_=gh.rearrange("(b p t) -> p b t", p=P, t=PACK))
         for b in range(1, HP):
             for a in range(KP):
                 load_w1(b, a, 1)
+        nc.sync.dma_start(out=board[:], in_=gy.rearrange("(p t) -> p t", t=PACK))
         nc.sync.dma_start(p1[:], pos1)
         nc.sync.dma_start(p2[:], pos2)
 
@@ -145,10 +144,10 @@ def tile_list_burst_quiet_board_kernel(
 
         act, h_b, h_q, h_s = {}, {}, {}, {}
 
-        def first_stage(b, s):
+        def first_stage(b, s, banks="acc"):
             act[b, s] = ring.tile([P, PACK, COLS], F32, name="act")
             for t in range(PACK):
-                acc = psum.tile([P, COLS], F32, name="acc")
+                acc = psum.tile([P, COLS], F32, name=banks)
                 for a in range(KP):
                     nc.tensor.matmul_mx(
                         out=acc[:],
@@ -161,14 +160,24 @@ def tile_list_burst_quiet_board_kernel(
                     )
                 nc.scalar.activation(out=act[b, s][:, t, :], in_=acc[:], func=ACT.Tanh, bias=bias[:, b, t : t + 1])
 
-        def round_h(b, s):
+        def round_h(b, s, on_vector=COLS):
             h_b[b, s] = ring.tile([P, PACK * COLS], BF16, name="h_b", align_bytes=64)
             nc.vector.tensor_tensor(
-                out=h_b[b, s][:].rearrange("p (c i t) -> p c t i", i=2, t=PACK),
-                in0=act[b, s][:].rearrange("p t (c i) -> p c t i", i=2),
-                in1=gain[:, b, :].unsqueeze(1).unsqueeze(3).broadcast_to([P, COLS // 2, PACK, 2]),
+                out=h_b[b, s][:, : PACK * on_vector].rearrange("p (c i t) -> p c t i", i=2, t=PACK),
+                in0=act[b, s][:, :, :on_vector].rearrange("p t (c i) -> p c t i", i=2),
+                in1=gain[:, b, :].unsqueeze(1).unsqueeze(3).broadcast_to([P, on_vector // 2, PACK, 2]),
                 op=ALU.mult,
             )
+            if on_vector < COLS:
+                planes = keep.tile([P, PACK, COLS - on_vector], BF16, name="planes")
+                for t in range(PACK):
+                    nc.scalar.activation(
+                        out=planes[:, t, :], in_=act[b, s][:, t, on_vector:], func=ACT.Copy, scale=gain[:, b, t : t + 1]
+                    )
+                nc.scalar.copy(
+                    out=h_b[b, s][:, PACK * on_vector :].rearrange("p (c i t) -> p c t i", i=4, t=PACK),
+                    in_=planes[:].rearrange("p t (c i) -> p c t i", i=4),
+                )
 
         def quantise_h(b, s):
             h_q[b, s] = keep.tile([P, COLS], U32, name=f"h_q{b}{s}", align_bytes=64)
@@ -179,7 +188,7 @@ def tile_list_burst_quiet_board_kernel(
 
         def second_stage(b, s, t):
             if b == 0:
-                score[s, t] = psum.tile([P, COLS], F32, name="score")
+                score[s, t] = psum.tile([P, COLS], F32, name="score" if s == 0 else "acc")
             nc.tensor.matmul_mx(
                 out=score[s, t][:],
                 lhsT=wa_w[:, b, 2 * t * P : 2 * (t + 1) * P].bitcast(FP4X4),
@@ -191,37 +200,41 @@ def tile_list_burst_quiet_board_kernel(
             )
 
         first_stage(0, 0)
+        first_stage(0, 1, "score")
         round_w1(1, 0, 2)
-        first_stage(0, 1)
         quantise_w1(1, 0)
-        round_h(0, 0)
-        round_w1(1, 1, 1)
-        quantise_h(0, 0)
-        round_w1(2, 0, 0)
+        round_w1(1, 1, 2)
         quantise_w1(1, 1)
-        round_h(0, 1)
         first_stage(1, 0)
-        for t in range(PACK):
-            second_stage(0, 0, t)
-        quantise_h(0, 1)
+        round_h(0, 0)
+        round_w1(2, 0, 0)
         round_w1(2, 1, 0)
-        quantise_w1(2, 0)
-        round_h(1, 0)
+        round_h(0, 1)
         first_stage(1, 1)
+        quantise_w1(2, 0)
+        quantise_h(0, 0)
+        quantise_h(0, 1)
+        round_h(1, 0)
         quantise_w1(2, 1)
-        quantise_h(1, 0)
         first_stage(2, 0)
-        for t in range(PACK):
-            second_stage(1, 0, t)
-        round_h(1, 1)
         first_stage(2, 1)
-        quantise_h(1, 1)
+        quantise_h(1, 0)
+        for b in range(HP - 1):
+            for t in range(PACK):
+                second_stage(b, 0, t)
+        round_h(1, 1)
         round_h(2, 0)
+        quantise_h(1, 1)
         quantise_h(2, 0)
         for t in range(PACK):
             second_stage(2, 0, t)
-        round_h(2, 1)
+        for b in range(HP - 1):
+            for t in range(PACK):
+                second_stage(b, 1, t)
+        round_h(2, 1, COLS // 2)
         quantise_h(2, 1)
+        for t in range(PACK):
+            second_stage(2, 1, t)
 
         e = [keep.tile([P, S], F32, name=f"e{t}") for t in range(PACK)]
         peak = keep.tile([P, SH, PACK], F32, name="peak")
@@ -240,8 +253,6 @@ def tile_list_burst_quiet_board_kernel(
 
         for t in range(PACK):
             keep_scores(0, t)
-            for b in range(HP):
-                second_stage(b, 1, t)
         for t in range(PACK):
             keep_scores(1, t)
             nc.scalar.mul(out=minus_peak[:, t : t + 1], in_=peak[:, SH - 1, t : t + 1], mul=-1.0)
@@ -254,26 +265,34 @@ def tile_list_burst_quiet_board_kernel(
             cols = slice(c * MC, (c + 1) * MC)
             entries = slice(c * MC // 16, (c + 1) * MC // 16)
             y = keep.tile([P, PACK, MC], F32, name=f"y{c}")
+            burst = keep.tile([P, PACK, MC], F32, name=f"burst{c}")
+            quiet = keep.tile([P, PACK, MC], F32, name=f"quiet{c}")
             for t in range(PACK):
-                burst = ring.tile([P, MC], F32, name="burst")
-                scaled = ring.tile([P, MC], F32, name="scaled")
                 nc.scalar.activation(
-                    out=burst[:], in_=e[t][:].indirect(p1[:, entries]), func=ACT.Exp, bias=minus_peak[:, t : t + 1]
+                    out=burst[:, t, :],
+                    in_=e[t][:].indirect(p1[:, entries]),
+                    func=ACT.Exp,
+                    bias=minus_peak[:, t : t + 1],
                 )
-                nc.scalar.activation(out=scaled[:], in_=burst[:], func=ACT.Copy, scale=board[:, t : t + 1])
-                nc.vector.tensor_tensor(
-                    out=y[:, t, :], in0=e[t][:].indirect(p2[:, entries]), in1=scaled[:], op=ALU.mult
+                nc.vector.tensor_copy(out=quiet[:, t, :], in_=e[t][:].indirect(p2[:, entries]))
+            for t in range(PACK):
+                nc.vector.scalar_tensor_tensor(
+                    out=y[:, t, :],
+                    in0=burst[:, t, :],
+                    scalar=board[:, t : t + 1],
+                    in1=quiet[:, t, :],
+                    op0=ALU.mult,
+                    op1=ALU.mult,
                 )
             nc.sync.dma_start(out=y_rows[:, :, cols], in_=y[:])
             y_b = keep.tile([P, PACK * MC], BF16, name=f"y_b{c}", align_bytes=64)
-            nc.vector.tensor_copy(
+            interleave = nc.scalar.copy if c == 0 else nc.vector.tensor_copy
+            interleave(
                 out=y_b[:].rearrange("p (c i t) -> p c t i", i=2, t=PACK),
                 in_=y[:].rearrange("p t (c i) -> p c t i", i=2),
             )
             nc.vector.quantize_mx(out=y_q[:, cols].bitcast(FP8X4), scales=y_s[:, cols], in_=y_b[:])
             nc.sync.dma_start(out=y_words[:, cols], in_=y_q[:, cols])
-        for q in range(QUADS):
-            queue = nc.sync if q % 2 == 0 else nc.scalar
-            queue.dma_start(
-                out=out_2[0, 4 * q : 4 * q + 4, :].bitcast(I32), in_=y_s[32 * q : 32 * q + 4, :].bitcast(I32)
-            )
+        for r in range(4):
+            queue = nc.sync if r % 2 == 0 else nc.scalar
+            queue.dma_start(out=out_2[0, r:16:4, :].bitcast(I32), in_=y_s[r:P:32, :].bitcast(I32))

@@ -42,16 +42,20 @@ def tile_list_burst_quiet_board_kernel(
         p1 = lists.tile([P, M // 16], U16, name="p1")
         p2 = lists.tile([P, M // 16], U16, name="p2")
 
-        tab_w = [keep.tile([P, T], I32, name=f"tab_w{a}") for a in range(KP)]
+        tab_w = [keep.tile([P, T], I32, name=f"tab_w{a}", align_bytes=64) for a in range(KP)]
         tab_s = keep.tile([P, T], U8, name="tab_s")
         wa_w_raw = keep.tile([P, HP, 2 * N], U8, name="wa_w_raw")
         wa_s_raw = keep.tile([P, HP, N], U8, name="wa_s_raw")
         wa_w = keep.tile([P, HP, 2 * N], U8, name="wa_w", align_bytes=64)
         wa_s = keep.tile([P, HP, N], U8, name="wa_s", align_bytes=64)
-        bias = keep.tile([P, HP, PACK], F32, name="bias")
-        gain = keep.tile([P, HP, PACK], F32, name="gain")
+        bias_0 = keep.tile([P, 1, PACK], F32, name="bias_0", align_bytes=64)
+        gain_0 = keep.tile([P, 1, PACK], F32, name="gain_0")
+        bias_r = keep.tile([P, HP - 1, PACK], F32, name="bias_r")
+        gain_r = keep.tile([P, HP - 1, PACK], F32, name="gain_r")
+        bias = [bias_0[:, 0, :]] + [bias_r[:, b, :] for b in range(HP - 1)]
+        gain = [gain_0[:, 0, :]] + [gain_r[:, b, :] for b in range(HP - 1)]
         board = keep.tile([P, PACK], F32, name="board")
-        w_raw = {(b, a): keep.tile([P, PACK, PASS], F32, name=f"w_raw{b}{a}") for b in range(HP) for a in range(KP)}
+        w_raw = {(b, a): keep.tile([P, PACK, PASS], F32, name=f"w_raw{b}{a}", align_bytes=64) for b in range(HP) for a in range(KP)}
 
         nc.vector.memset(tab_s[:].bitcast(I32), 0)
         nc.vector.memset(wa_s_raw[:].bitcast(I32), 0)
@@ -62,15 +66,19 @@ def tile_list_burst_quiet_board_kernel(
             for j in range(0, PACK, step):
                 nc.sync.dma_start(out=w_raw[b, a][:, j : j + step, :], in_=rows[:, j : j + step, :])
 
+        def load_tab_words(a, half):
+            words = tab_words[a].rearrange("p t i -> p (t i)").bitcast(I32)
+            cols = slice(half * T // 2, (half + 1) * T // 2)
+            nc.sync.dma_start(out=tab_w[a][:, cols], in_=words[:, cols])
+
+        def load_vector(tile, vector, blocks):
+            nc.sync.dma_start(out=tile[:], in_=vector.rearrange("(b p t) -> p b t", p=P, t=PACK)[:, blocks, :])
+
         def load_tab_scales(a, r):
             nc.sync.dma_start(
                 out=tab_s[4 * a + r : P : 32, :].bitcast(I32),
                 in_=tab_scales[a, r : 16 : 4, :].bitcast(I32),
             )
-
-        def load_tab_words(a, cols):
-            words = tab_words[a].rearrange("p t i -> p (t i)").bitcast(I32)
-            nc.sync.dma_start(out=tab_w[a][:, cols], in_=words[:, cols])
 
         nc.sync.dma_start(idx[:], offs)
         load_w1(0, 0, 4)
@@ -79,31 +87,35 @@ def tile_list_burst_quiet_board_kernel(
         nc.sync.dma_start(out=wa_w_raw[:, 2:, :].bitcast(I32), in_=wa_rows[:, 2:, :])
         load_w1(0, 1, 1)
         scale_rows = [(a, r) for r in range(4) for a in range(KP)]
-        for a, q in scale_rows[:6]:
-            load_tab_scales(a, q)
-        load_tab_words(0, slice(0, T // 2))
-        for a, q in scale_rows[6:]:
-            load_tab_scales(a, q)
+        for a, r in scale_rows[:6]:
+            load_tab_scales(a, r)
+        load_tab_words(0, 0)
+        for a, r in scale_rows[6:]:
+            load_tab_scales(a, r)
         for r in range(4):
             nc.sync.dma_start(
                 out=wa_s_raw[r:P:32, :, :].bitcast(I32),
                 in_=wa_scales[:, r:16:4, :].rearrange("a q n -> q a n").bitcast(I32),
             )
-        load_tab_words(0, slice(T // 2, T))
-        load_tab_words(1, slice(0, T))
-        nc.sync.dma_start(out=bias[:], in_=b1.rearrange("(b p t) -> p b t", p=P, t=PACK))
-        nc.sync.dma_start(out=gain[:], in_=gh.rearrange("(b p t) -> p b t", p=P, t=PACK))
-        for b in range(1, HP):
-            for a in range(KP):
-                load_w1(b, a, 1)
+        load_tab_words(0, 1)
+        load_tab_words(1, 0)
+        load_tab_words(1, 1)
+        load_vector(bias_0, b1, slice(0, 1))
+        load_w1(1, 0, 1)
+        load_vector(gain_0, gh, slice(0, 1))
+        load_w1(1, 1, 1)
+        load_vector(bias_r, b1, slice(1, HP))
+        load_vector(gain_r, gh, slice(1, HP))
+        load_w1(2, 0, 1)
+        load_w1(2, 1, 1)
         nc.sync.dma_start(out=board[:], in_=gy.rearrange("(p t) -> p t", t=PACK))
         nc.sync.dma_start(p1[:], pos1)
         nc.sync.dma_start(p2[:], pos2)
 
         w_b, w_q, w_s = {}, {}, {}
 
-        def round_w1(b, a, on_vector):
-            w_b[b, a] = ring.tile([P, PACK * PASS], BF16, name="w_b", align_bytes=64)
+        def round_w1(b, a, on_vector, slot):
+            w_b[b, a] = keep.tile([P, PACK * PASS], BF16, name=f"w_b{b}{a}", tag=slot, align_bytes=64)
             dst = w_b[b, a][:].rearrange("p (g u m j) -> p g m j u", g=2, u=2, j=PACK)
             src = w_raw[b, a][:].rearrange("p j (m g u) -> p g m j u", g=2, u=2)
             if on_vector == 2:
@@ -119,33 +131,32 @@ def tile_list_burst_quiet_board_kernel(
             w_s[b, a] = keep.tile([P, PASS], U8, name=f"w_s{b}{a}", align_bytes=64)
             nc.vector.quantize_mx(out=w_q[b, a][:].bitcast(FP8X4), scales=w_s[b, a][:], in_=w_b[b, a][:])
 
-        round_w1(0, 0, 0)
-        round_w1(0, 1, 0)
-        quantise_w1(0, 0)
-        nc.vector.tensor_copy(
+        round_w1(0, 0, 0, "w_b00")
+        round_w1(0, 1, 0, "w_b01")
+        nc.scalar.copy(
             out=wa_w[:].bitcast(U16).rearrange("p a (t m) -> p a m t", t=PACK),
             in_=wa_w_raw[:].bitcast(U16).rearrange("p a (m t) -> p a m t", t=PACK),
         )
-        quantise_w1(0, 1)
+        nc.gpsimd.tensor_copy(
+            out=wa_s[:].rearrange("p a (t m) -> p a t m", t=PACK),
+            in_=wa_s_raw[:].rearrange("p a (m t) -> p a t m", t=PACK),
+        )
 
         v_s = keep.tile([P, S], U8, name="v_s", align_bytes=64)
         nc.vector.tensor_copy(out=v_s[:], in_=tab_s[:].indirect(idx[:]))
+        quantise_w1(0, 0)
+        quantise_w1(0, 1)
         v_w = {}
         for a in range(KP):
             for s in range(SH):
                 v_w[a, s] = keep.tile([P, COLS], U32, name=f"v_w{a}{s}", align_bytes=64)
                 entries = idx[:, s * COLS // 16 : (s + 1) * COLS // 16]
                 nc.vector.tensor_copy(out=v_w[a, s][:], in_=tab_w[a][:].bitcast(U32).indirect(entries))
-            if a == 0:
-                nc.vector.tensor_copy(
-                    out=wa_s[:].rearrange("p a (t m) -> p a m t", t=PACK),
-                    in_=wa_s_raw[:].rearrange("p a (m t) -> p a m t", t=PACK),
-                )
 
         act, h_b, h_q, h_s = {}, {}, {}, {}
 
-        def first_stage(b, s, banks="acc"):
-            act[b, s] = ring.tile([P, PACK, COLS], F32, name="act")
+        def first_stage(b, s, slot, banks="acc"):
+            act[b, s] = keep.tile([P, PACK, COLS], F32, name=f"act{b}{s}", tag=slot, align_bytes=64)
             for t in range(PACK):
                 acc = psum.tile([P, COLS], F32, name=banks)
                 for a in range(KP):
@@ -158,21 +169,21 @@ def tile_list_burst_quiet_board_kernel(
                         start=(a == 0),
                         stop=(a == KP - 1),
                     )
-                nc.scalar.activation(out=act[b, s][:, t, :], in_=acc[:], func=ACT.Tanh, bias=bias[:, b, t : t + 1])
+                nc.scalar.activation(out=act[b, s][:, t, :], in_=acc[:], func=ACT.Tanh, bias=bias[b][:, t : t + 1])
 
         def round_h(b, s, on_vector=COLS):
-            h_b[b, s] = ring.tile([P, PACK * COLS], BF16, name="h_b", align_bytes=64)
+            h_b[b, s] = keep.tile([P, PACK * COLS], BF16, name=f"h_b{b}{s}", tag=f"w_b0{s}", align_bytes=64)
             nc.vector.tensor_tensor(
                 out=h_b[b, s][:, : PACK * on_vector].rearrange("p (c i t) -> p c t i", i=2, t=PACK),
                 in0=act[b, s][:, :, :on_vector].rearrange("p t (c i) -> p c t i", i=2),
-                in1=gain[:, b, :].unsqueeze(1).unsqueeze(3).broadcast_to([P, on_vector // 2, PACK, 2]),
+                in1=gain[b].unsqueeze(1).unsqueeze(3).broadcast_to([P, on_vector // 2, PACK, 2]),
                 op=ALU.mult,
             )
             if on_vector < COLS:
                 planes = keep.tile([P, PACK, COLS - on_vector], BF16, name="planes")
                 for t in range(PACK):
                     nc.scalar.activation(
-                        out=planes[:, t, :], in_=act[b, s][:, t, on_vector:], func=ACT.Copy, scale=gain[:, b, t : t + 1]
+                        out=planes[:, t, :], in_=act[b, s][:, t, on_vector:], func=ACT.Copy, scale=gain[b][:, t : t + 1]
                     )
                 nc.scalar.copy(
                     out=h_b[b, s][:, PACK * on_vector :].rearrange("p (c i t) -> p c t i", i=4, t=PACK),
@@ -188,7 +199,7 @@ def tile_list_burst_quiet_board_kernel(
 
         def second_stage(b, s, t):
             if b == 0:
-                score[s, t] = psum.tile([P, COLS], F32, name="score" if s == 0 else "acc")
+                score[s, t] = psum.tile([P, COLS], F32, name="acc" if s == 0 else "score")
             nc.tensor.matmul_mx(
                 out=score[s, t][:],
                 lhsT=wa_w[:, b, 2 * t * P : 2 * (t + 1) * P].bitcast(FP4X4),
@@ -199,39 +210,39 @@ def tile_list_burst_quiet_board_kernel(
                 stop=(b == HP - 1),
             )
 
-        first_stage(0, 0)
-        first_stage(0, 1, "score")
-        round_w1(1, 0, 2)
+        first_stage(0, 0, "act_a")
+        first_stage(0, 1, "act_b")
+        round_w1(1, 0, 2, "tab_w1")
         quantise_w1(1, 0)
-        round_w1(1, 1, 2)
+        round_w1(1, 1, 2, "w_b00")
         quantise_w1(1, 1)
-        first_stage(1, 0)
+        first_stage(1, 0, "tab_w0")
         round_h(0, 0)
-        round_w1(2, 0, 0)
-        round_w1(2, 1, 0)
+        round_w1(2, 0, 0, "bias_0")
         round_h(0, 1)
-        first_stage(1, 1)
-        quantise_w1(2, 0)
+        round_w1(2, 1, 0, "act_b")
+        first_stage(1, 1, "tab_w1", "score")
         quantise_h(0, 0)
+        quantise_w1(2, 0)
         quantise_h(0, 1)
         round_h(1, 0)
         quantise_w1(2, 1)
-        first_stage(2, 0)
-        first_stage(2, 1)
+        first_stage(2, 0, "act_a")
+        first_stage(2, 1, "act_b", "score")
         quantise_h(1, 0)
         for b in range(HP - 1):
             for t in range(PACK):
                 second_stage(b, 0, t)
         round_h(1, 1)
         round_h(2, 0)
-        quantise_h(1, 1)
         quantise_h(2, 0)
+        quantise_h(1, 1)
         for t in range(PACK):
             second_stage(2, 0, t)
         for b in range(HP - 1):
             for t in range(PACK):
                 second_stage(b, 1, t)
-        round_h(2, 1, COLS // 2)
+        round_h(2, 1, 3 * COLS // 8)
         quantise_h(2, 1)
         for t in range(PACK):
             second_stage(2, 1, t)
@@ -265,29 +276,19 @@ def tile_list_burst_quiet_board_kernel(
             cols = slice(c * MC, (c + 1) * MC)
             entries = slice(c * MC // 16, (c + 1) * MC // 16)
             y = keep.tile([P, PACK, MC], F32, name=f"y{c}")
-            burst = keep.tile([P, PACK, MC], F32, name=f"burst{c}")
-            quiet = keep.tile([P, PACK, MC], F32, name=f"quiet{c}")
             for t in range(PACK):
+                burst = ring.tile([P, MC], F32, name="burst")
+                scaled = ring.tile([P, MC], F32, name="scaled")
                 nc.scalar.activation(
-                    out=burst[:, t, :],
-                    in_=e[t][:].indirect(p1[:, entries]),
-                    func=ACT.Exp,
-                    bias=minus_peak[:, t : t + 1],
+                    out=burst[:], in_=e[t][:].indirect(p1[:, entries]), func=ACT.Exp, bias=minus_peak[:, t : t + 1]
                 )
-                nc.vector.tensor_copy(out=quiet[:, t, :], in_=e[t][:].indirect(p2[:, entries]))
-            for t in range(PACK):
-                nc.vector.scalar_tensor_tensor(
-                    out=y[:, t, :],
-                    in0=burst[:, t, :],
-                    scalar=board[:, t : t + 1],
-                    in1=quiet[:, t, :],
-                    op0=ALU.mult,
-                    op1=ALU.mult,
+                nc.scalar.activation(out=scaled[:], in_=burst[:], func=ACT.Copy, scale=board[:, t : t + 1])
+                nc.vector.tensor_tensor(
+                    out=y[:, t, :], in0=e[t][:].indirect(p2[:, entries]), in1=scaled[:], op=ALU.mult
                 )
             nc.sync.dma_start(out=y_rows[:, :, cols], in_=y[:])
             y_b = keep.tile([P, PACK * MC], BF16, name=f"y_b{c}", align_bytes=64)
-            interleave = nc.scalar.copy if c == 0 else nc.vector.tensor_copy
-            interleave(
+            nc.vector.tensor_copy(
                 out=y_b[:].rearrange("p (c i t) -> p c t i", i=2, t=PACK),
                 in_=y[:].rearrange("p t (c i) -> p c t i", i=2),
             )

@@ -35,7 +35,6 @@ def tile_list_burst_quiet_board_kernel(
     with ExitStack() as ctx:
         lists = ctx.enter_context(tc.tile_pool(name="lists", bufs=1))
         keep = ctx.enter_context(tc.tile_pool(name="keep", bufs=1))
-        ring = ctx.enter_context(tc.tile_pool(name="ring", bufs=3))
         psum = ctx.enter_context(tc.psum_pool(name="psum", bufs=4))
 
         idx = lists.tile([P, S // 16], U16, name="idx")
@@ -102,12 +101,12 @@ def tile_list_burst_quiet_board_kernel(
         load_tab_words(1, 1)
         load_vector(bias_0, b1, slice(0, 1))
         load_w1(1, 0, 1)
-        load_vector(gain_0, gh, slice(0, 1))
         load_w1(1, 1, 1)
-        load_vector(bias_r, b1, slice(1, HP))
-        load_vector(gain_r, gh, slice(1, HP))
+        load_vector(gain_0, gh, slice(0, 1))
         load_w1(2, 0, 1)
+        load_vector(bias_r, b1, slice(1, HP))
         load_w1(2, 1, 1)
+        load_vector(gain_r, gh, slice(1, HP))
         nc.sync.dma_start(out=board[:], in_=gy.rearrange("(p t) -> p t", t=PACK))
         nc.sync.dma_start(p1[:], pos1)
         nc.sync.dma_start(p2[:], pos2)
@@ -171,8 +170,8 @@ def tile_list_burst_quiet_board_kernel(
                     )
                 nc.scalar.activation(out=act[b, s][:, t, :], in_=acc[:], func=ACT.Tanh, bias=bias[b][:, t : t + 1])
 
-        def round_h(b, s, on_vector=COLS):
-            h_b[b, s] = keep.tile([P, PACK * COLS], BF16, name=f"h_b{b}{s}", tag=f"w_b0{s}", align_bytes=64)
+        def round_h(b, s, slot, on_vector=COLS):
+            h_b[b, s] = keep.tile([P, PACK * COLS], BF16, name=f"h_b{b}{s}", tag=slot, align_bytes=64)
             nc.vector.tensor_tensor(
                 out=h_b[b, s][:, : PACK * on_vector].rearrange("p (c i t) -> p c t i", i=2, t=PACK),
                 in0=act[b, s][:, :, :on_vector].rearrange("p t (c i) -> p c t i", i=2),
@@ -216,16 +215,16 @@ def tile_list_burst_quiet_board_kernel(
         quantise_w1(1, 0)
         round_w1(1, 1, 2, "w_b00")
         quantise_w1(1, 1)
-        first_stage(1, 0, "tab_w0")
-        round_h(0, 0)
         round_w1(2, 0, 0, "bias_0")
-        round_h(0, 1)
+        first_stage(1, 0, "w_raw20")
+        round_h(0, 0, "w_b00")
+        round_h(0, 1, "act_a")
         round_w1(2, 1, 0, "act_b")
-        first_stage(1, 1, "tab_w1", "score")
+        first_stage(1, 1, "w_raw21", "score")
         quantise_h(0, 0)
         quantise_w1(2, 0)
         quantise_h(0, 1)
-        round_h(1, 0)
+        round_h(1, 0, "w_b00")
         quantise_w1(2, 1)
         first_stage(2, 0, "act_a")
         first_stage(2, 1, "act_b", "score")
@@ -233,8 +232,8 @@ def tile_list_burst_quiet_board_kernel(
         for b in range(HP - 1):
             for t in range(PACK):
                 second_stage(b, 0, t)
-        round_h(1, 1)
-        round_h(2, 0)
+        round_h(1, 1, "w_b01")
+        round_h(2, 0, "w_b00")
         quantise_h(2, 0)
         quantise_h(1, 1)
         for t in range(PACK):
@@ -242,7 +241,7 @@ def tile_list_burst_quiet_board_kernel(
         for b in range(HP - 1):
             for t in range(PACK):
                 second_stage(b, 1, t)
-        round_h(2, 1, 3 * COLS // 8)
+        round_h(2, 1, "w_b01", COLS // 2)
         quantise_h(2, 1)
         for t in range(PACK):
             second_stage(2, 1, t)
@@ -272,23 +271,29 @@ def tile_list_burst_quiet_board_kernel(
         y_s = keep.tile([P, M], U8, name="y_s", align_bytes=64)
         y_rows = out_0.rearrange("(p t) m -> p t m", t=PACK)
         y_words = out_1[0].rearrange("p m t -> p (m t)").bitcast(I32)
+        burst = keep.tile([P, PACK, M], F32, name="burst")
+        quiet = keep.tile([P, PACK, M], F32, name="quiet")
+        for t in range(PACK):
+            nc.scalar.activation(
+                out=burst[:, t, :], in_=e[t][:].indirect(p1[:]), func=ACT.Exp, bias=minus_peak[:, t : t + 1]
+            )
+            nc.vector.tensor_copy(out=quiet[:, t, :], in_=e[t][:].indirect(p2[:]))
         for c in range(MH):
             cols = slice(c * MC, (c + 1) * MC)
-            entries = slice(c * MC // 16, (c + 1) * MC // 16)
             y = keep.tile([P, PACK, MC], F32, name=f"y{c}")
             for t in range(PACK):
-                burst = ring.tile([P, MC], F32, name="burst")
-                scaled = ring.tile([P, MC], F32, name="scaled")
-                nc.scalar.activation(
-                    out=burst[:], in_=e[t][:].indirect(p1[:, entries]), func=ACT.Exp, bias=minus_peak[:, t : t + 1]
-                )
-                nc.scalar.activation(out=scaled[:], in_=burst[:], func=ACT.Copy, scale=board[:, t : t + 1])
-                nc.vector.tensor_tensor(
-                    out=y[:, t, :], in0=e[t][:].indirect(p2[:, entries]), in1=scaled[:], op=ALU.mult
+                nc.vector.scalar_tensor_tensor(
+                    out=y[:, t, :],
+                    in0=burst[:, t, cols],
+                    scalar=board[:, t : t + 1],
+                    in1=quiet[:, t, cols],
+                    op0=ALU.mult,
+                    op1=ALU.mult,
                 )
             nc.sync.dma_start(out=y_rows[:, :, cols], in_=y[:])
             y_b = keep.tile([P, PACK * MC], BF16, name=f"y_b{c}", align_bytes=64)
-            nc.vector.tensor_copy(
+            interleave = nc.scalar.copy if c == 0 else nc.vector.tensor_copy
+            interleave(
                 out=y_b[:].rearrange("p (c i t) -> p c t i", i=2, t=PACK),
                 in_=y[:].rearrange("p t (c i) -> p c t i", i=2),
             )

from contextlib import ExitStack

import concourse.mybir as mybir

K, T, S, H, N, M = 1024, 4096, 1024, 1536, 512, 512
FLOPS = 2 * K * H * S + 2 * H * N * S

F32 = mybir.dt.float32
BF16 = mybir.dt.bfloat16
I32 = mybir.dt.int32
U32 = mybir.dt.uint32
U16 = mybir.dt.uint16
U8 = mybir.dt.uint8
FP8X4 = mybir.dt.float8_e4m3fn_x4
FP4X4 = mybir.dt.float4_e2m1fn_x4
ALU = mybir.AluOpType
ACT = mybir.ActivationFunctionType

P = 128
PACK = 4
PASS = P * PACK
KP = K // PASS
HP = H // PASS
COLS = 512
SH = S // COLS
MC = 256
MH = M // MC
QUADS = 4


def tile_list_burst_quiet_board_kernel(
    tc, tab_words, tab_scales, offs, w1, b1, gh, wa_words, wa_scales, pos1, pos2, gy, out_0, out_1, out_2
):
    nc = tc.nc
    with ExitStack() as ctx:
        lists = ctx.enter_context(tc.tile_pool(name="lists", bufs=1))
        keep = ctx.enter_context(tc.tile_pool(name="keep", bufs=1))
        psum = ctx.enter_context(tc.psum_pool(name="psum", bufs=4))

        idx = lists.tile([P, S // 16], U16, name="idx")
        p1 = lists.tile([P, M // 16], U16, name="p1")
        p2 = lists.tile([P, M // 16], U16, name="p2")

        tab_w = [keep.tile([P, T], I32, name=f"tab_w{a}", align_bytes=64) for a in range(KP)]
        tab_s = keep.tile([P, T], U8, name="tab_s")
        wa_w_raw = keep.tile([P, HP, 2 * N], U8, name="wa_w_raw")
        wa_s_raw = keep.tile([P, HP, N], U8, name="wa_s_raw")
        wa_w = keep.tile([P, HP, 2 * N], U8, name="wa_w", align_bytes=64)
        wa_s = keep.tile([P, HP, N], U8, name="wa_s", align_bytes=64)
        bias_0 = keep.tile([P, 1, PACK], F32, name="bias_0", align_bytes=64)
        gain_0 = keep.tile([P, 1, PACK], F32, name="gain_0")
        bias_r = keep.tile([P, HP - 1, PACK], F32, name="bias_r")
        gain_r = keep.tile([P, HP - 1, PACK], F32, name="gain_r")
        bias = [bias_0[:, 0, :]] + [bias_r[:, b, :] for b in range(HP - 1)]
        gain = [gain_0[:, 0, :]] + [gain_r[:, b, :] for b in range(HP - 1)]
        board = keep.tile([P, PACK], F32, name="board")
        w_raw = {(b, a): keep.tile([P, PACK, PASS], F32, name=f"w_raw{b}{a}", align_bytes=64) for b in range(HP) for a in range(KP)}

        nc.vector.memset(tab_s[:].bitcast(I32), 0)
        nc.vector.memset(wa_s_raw[:].bitcast(I32), 0)

        def load_w1(b, a, pieces):
            rows = w1[a * PASS : (a + 1) * PASS, b * PASS : (b + 1) * PASS].rearrange("(p j) c -> p j c", j=PACK)
            step = PACK // pieces
            for j in range(0, PACK, step):
                nc.sync.dma_start(out=w_raw[b, a][:, j : j + step, :], in_=rows[:, j : j + step, :])

        def load_tab_words(a, half):
            words = tab_words[a].rearrange("p t i -> p (t i)").bitcast(I32)
            cols = slice(half * T // 2, (half + 1) * T // 2)
            nc.sync.dma_start(out=tab_w[a][:, cols], in_=words[:, cols])

        def load_vector(tile, vector, blocks):
            nc.sync.dma_start(out=tile[:], in_=vector.rearrange("(b p t) -> p b t", p=P, t=PACK)[:, blocks, :])

        def load_tab_scales(a, r):
            nc.sync.dma_start(
                out=tab_s[4 * a + r : P : 32, :].bitcast(I32),
                in_=tab_scales[a, r : 16 : 4, :].bitcast(I32),
            )

        nc.sync.dma_start(idx[:], offs)
        load_w1(0, 0, 4)
        wa_rows = wa_words.rearrange("a p c -> p a c").bitcast(I32)
        nc.sync.dma_start(out=wa_w_raw[:, :2, :].bitcast(I32), in_=wa_rows[:, :2, :])
        nc.sync.dma_start(out=wa_w_raw[:, 2:, :].bitcast(I32), in_=wa_rows[:, 2:, :])
        load_w1(0, 1, 1)
        scale_rows = [(a, r) for r in range(4) for a in range(KP)]
        for a, r in scale_rows[:6]:
            load_tab_scales(a, r)
        load_tab_words(0, 0)
        for a, r in scale_rows[6:]:
            load_tab_scales(a, r)
        for r in range(4):
            nc.sync.dma_start(
                out=wa_s_raw[r:P:32, :, :].bitcast(I32),
                in_=wa_scales[:, r:16:4, :].rearrange("a q n -> q a n").bitcast(I32),
            )
        load_tab_words(0, 1)
        load_tab_words(1, 0)
        load_tab_words(1, 1)
        load_vector(bias_0, b1, slice(0, 1))
        load_w1(1, 0, 1)
        load_w1(1, 1, 1)
        load_vector(gain_0, gh, slice(0, 1))
        load_w1(2, 0, 1)
        load_vector(bias_r, b1, slice(1, HP))
        load_w1(2, 1, 1)
        load_vector(gain_r, gh, slice(1, HP))
        nc.sync.dma_start(out=board[:], in_=gy.rearrange("(p t) -> p t", t=PACK))
        nc.sync.dma_start(p1[:], pos1)
        nc.sync.dma_start(p2[:], pos2)

        w_b, w_q, w_s = {}, {}, {}

        def round_w1(b, a, on_vector, slot):
            w_b[b, a] = keep.tile([P, PACK * PASS], BF16, name=f"w_b{b}{a}", tag=slot, align_bytes=64)
            dst = w_b[b, a][:].rearrange("p (g u m j) -> p g m j u", g=2, u=2, j=PACK)
            src = w_raw[b, a][:].rearrange("p j (m g u) -> p g m j u", g=2, u=2)
            if on_vector == 2:
                nc.vector.tensor_copy(out=dst, in_=src)
            elif on_vector == 1:
                nc.vector.tensor_copy(out=dst[:, 0], in_=src[:, 0])
                nc.scalar.copy(out=dst[:, 1], in_=src[:, 1])
            else:
                nc.scalar.copy(out=dst, in_=src)

        def quantise_w1(b, a):
            w_q[b, a] = keep.tile([P, PASS], U32, name=f"w_q{b}{a}", align_bytes=64)
            w_s[b, a] = keep.tile([P, PASS], U8, name=f"w_s{b}{a}", align_bytes=64)
            nc.vector.quantize_mx(out=w_q[b, a][:].bitcast(FP8X4), scales=w_s[b, a][:], in_=w_b[b, a][:])

        round_w1(0, 0, 0, "w_b00")
        round_w1(0, 1, 0, "w_b01")
        nc.scalar.copy(
            out=wa_w[:].bitcast(U16).rearrange("p a (t m) -> p a m t", t=PACK),
            in_=wa_w_raw[:].bitcast(U16).rearrange("p a (m t) -> p a m t", t=PACK),
        )
        nc.gpsimd.tensor_copy(
            out=wa_s[:].rearrange("p a (t m) -> p a t m", t=PACK),
            in_=wa_s_raw[:].rearrange("p a (m t) -> p a t m", t=PACK),
        )

        v_s = keep.tile([P, S], U8, name="v_s", align_bytes=64)
        nc.vector.tensor_copy(out=v_s[:], in_=tab_s[:].indirect(idx[:]))
        quantise_w1(0, 0)
        quantise_w1(0, 1)
        v_w = {}
        for a in range(KP):
            for s in range(SH):
                v_w[a, s] = keep.tile([P, COLS], U32, name=f"v_w{a}{s}", align_bytes=64)
                entries = idx[:, s * COLS // 16 : (s + 1) * COLS // 16]
                nc.vector.tensor_copy(out=v_w[a, s][:], in_=tab_w[a][:].bitcast(U32).indirect(entries))

        act, h_b, h_q, h_s = {}, {}, {}, {}

        def first_stage(b, s, slot, banks="acc"):
            act[b, s] = keep.tile([P, PACK, COLS], F32, name=f"act{b}{s}", tag=slot, align_bytes=64)
            for t in range(PACK):
                acc = psum.tile([P, COLS], F32, name=banks)
                for a in range(KP):
                    nc.tensor.matmul_mx(
                        out=acc[:],
                        lhsT=w_q[b, a][:, t * P : (t + 1) * P].bitcast(FP8X4),
                        lhsT_scale=w_s[b, a][:, t * P : (t + 1) * P],
                        rhs=v_w[a, s][:].bitcast(FP8X4),
                        rhs_scale=v_s[4 * a : P, s * COLS : (s + 1) * COLS],
                        start=(a == 0),
                        stop=(a == KP - 1),
                    )
                nc.scalar.activation(out=act[b, s][:, t, :], in_=acc[:], func=ACT.Tanh, bias=bias[b][:, t : t + 1])

        def round_h(b, s, slot, on_vector=COLS):
            h_b[b, s] = keep.tile([P, PACK * COLS], BF16, name=f"h_b{b}{s}", tag=slot, align_bytes=64)
            nc.vector.tensor_tensor(
                out=h_b[b, s][:, : PACK * on_vector].rearrange("p (c i t) -> p c t i", i=2, t=PACK),
                in0=act[b, s][:, :, :on_vector].rearrange("p t (c i) -> p c t i", i=2),
                in1=gain[b].unsqueeze(1).unsqueeze(3).broadcast_to([P, on_vector // 2, PACK, 2]),
                op=ALU.mult,
            )
            if on_vector < COLS:
                planes = keep.tile([P, PACK, COLS - on_vector], BF16, name="planes")
                for t in range(PACK):
                    nc.scalar.activation(
                        out=planes[:, t, :], in_=act[b, s][:, t, on_vector:], func=ACT.Copy, scale=gain[b][:, t : t + 1]
                    )
                nc.scalar.copy(
                    out=h_b[b, s][:, PACK * on_vector :].rearrange("p (c i t) -> p c t i", i=4, t=PACK),
                    in_=planes[:].rearrange("p t (c i) -> p c t i", i=4),
                )

        def quantise_h(b, s):
            h_q[b, s] = keep.tile([P, COLS], U32, name=f"h_q{b}{s}", align_bytes=64)
            h_s[b, s] = keep.tile([P, COLS], U8, name=f"h_s{b}{s}", align_bytes=64)
            nc.vector.quantize_mx(out=h_q[b, s][:].bitcast(FP8X4), scales=h_s[b, s][:], in_=h_b[b, s][:])

        score = {}

        def second_stage(b, s, t):
            if b == 0:
                score[s, t] = psum.tile([P, COLS], F32, name="acc" if s == 0 else "score")
            nc.tensor.matmul_mx(
                out=score[s, t][:],
                lhsT=wa_w[:, b, 2 * t * P : 2 * (t + 1) * P].bitcast(FP4X4),
                lhsT_scale=wa_s[:, b, t * P : (t + 1) * P],
                rhs=h_q[b, s][:].bitcast(FP8X4),
                rhs_scale=h_s[b, s][:],
                start=(b == 0),
                stop=(b == HP - 1),
            )

        first_stage(0, 0, "act_a")
        first_stage(0, 1, "act_b")
        round_w1(1, 0, 2, "tab_w1")
        quantise_w1(1, 0)
        round_w1(1, 1, 2, "w_b00")
        quantise_w1(1, 1)
        round_w1(2, 0, 0, "bias_0")
        first_stage(1, 0, "w_raw20")
        round_h(0, 0, "w_b00")
        round_h(0, 1, "act_a")
        round_w1(2, 1, 0, "act_b")
        first_stage(1, 1, "w_raw21", "score")
        quantise_h(0, 0)
        quantise_w1(2, 0)
        quantise_h(0, 1)
        round_h(1, 0, "w_b00")
        quantise_w1(2, 1)
        first_stage(2, 0, "act_a")
        first_stage(2, 1, "act_b", "score")
        quantise_h(1, 0)
        for b in range(HP - 1):
            for t in range(PACK):
                second_stage(b, 0, t)
        round_h(1, 1, "w_b01")
        round_h(2, 0, "w_b00")
        quantise_h(2, 0)
        quantise_h(1, 1)
        for t in range(PACK):
            second_stage(2, 0, t)
        for b in range(HP - 1):
            for t in range(PACK):
                second_stage(b, 1, t)
        round_h(2, 1, "w_b01", COLS // 2)
        quantise_h(2, 1)
        for t in range(PACK):
            second_stage(2, 1, t)

        e = [keep.tile([P, S], F32, name=f"e{t}") for t in range(PACK)]
        peak = keep.tile([P, SH, PACK], F32, name="peak")
        minus_peak = keep.tile([P, PACK], F32, name="minus_peak")

        def keep_scores(s, t):
            nc.vector.tensor_scalar(
                out=e[t][:, s * COLS : (s + 1) * COLS],
                in0=score[s, t][:],
                scalar1=1.0,
                scalar2=None if s == 0 else peak[:, s - 1, t : t + 1],
                op0=ALU.mult,
                op1=ALU.max,
                accum_out=peak[:, s, t : t + 1],
            )

        for t in range(PACK):
            keep_scores(0, t)
        for t in range(PACK):
            keep_scores(1, t)
            nc.scalar.mul(out=minus_peak[:, t : t + 1], in_=peak[:, SH - 1, t : t + 1], mul=-1.0)

        y_q = keep.tile([P, M], I32, name="y_q", align_bytes=64)
        y_s = keep.tile([P, M], U8, name="y_s", align_bytes=64)
        y_rows = out_0.rearrange("(p t) m -> p t m", t=PACK)
        y_words = out_1[0].rearrange("p m t -> p (m t)").bitcast(I32)
        burst = keep.tile([P, PACK, M], F32, name="burst")
        quiet = keep.tile([P, PACK, M], F32, name="quiet")
        for t in range(PACK):
            nc.scalar.activation(
                out=burst[:, t, :], in_=e[t][:].indirect(p1[:]), func=ACT.Exp, bias=minus_peak[:, t : t + 1]
            )
            nc.vector.tensor_copy(out=quiet[:, t, :], in_=e[t][:].indirect(p2[:]))
        for c in range(MH):
            cols = slice(c * MC, (c + 1) * MC)
            y = keep.tile([P, PACK, MC], F32, name=f"y{c}")
            for t in range(PACK):
                nc.vector.scalar_tensor_tensor(
                    out=y[:, t, :],
                    in0=burst[:, t, cols],
                    scalar=board[:, t : t + 1],
                    in1=quiet[:, t, cols],
                    op0=ALU.mult,
                    op1=ALU.mult,
                )
            nc.sync.dma_start(out=y_rows[:, :, cols], in_=y[:])
            y_b = keep.tile([P, PACK * MC], BF16, name=f"y_b{c}", align_bytes=64)
            interleave = nc.scalar.copy if c == 0 else nc.vector.tensor_copy
            interleave(
                out=y_b[:].rearrange("p (c i t) -> p c t i", i=2, t=PACK),
                in_=y[:].rearrange("p t (c i) -> p c t i", i=2),
            )
            nc.vector.quantize_mx(out=y_q[:, cols].bitcast(FP8X4), scales=y_s[:, cols], in_=y_b[:])
            nc.sync.dma_start(out=y_words[:, cols], in_=y_q[:, cols])
        for r in range(4):
            queue = nc.sync if r % 2 == 0 else nc.scalar
            queue.dma_start(out=out_2[0, r:16:4, :].bitcast(I32), in_=y_s[r:P:32, :].bitcast(I32))
